import numpy as np
import ml_dtypes


def mxq(x, axis, fmt="e4m3"):
    dtype, down = {"e4m3": (ml_dtypes.float8_e4m3fn, 7), "e5m2": (ml_dtypes.float8_e5m2, 14)}[fmt]
    v = np.moveaxis(np.asarray(x, np.float32).astype(ml_dtypes.bfloat16).astype(np.float64), axis, -1)
    blocks = v.reshape(v.shape[:-1] + (-1, 32))
    amax = np.abs(blocks).max(-1, keepdims=True)
    byte = np.maximum(np.where(amax > 0, np.frexp(amax)[1] - 1 + 127, 0) - down, 1)
    scale = np.exp2(byte - 127.0)
    codes = (blocks / scale).astype(np.float32).astype(dtype).astype(np.float64)
    return np.moveaxis((codes * scale).reshape(v.shape), -1, axis)


WIDE = False


def mx_kscale(k):
    if not WIDE:
        return np.ones(k)
    levels = np.array([10, -10, 5, -5, 0])
    if k % 512:
        return np.exp2(np.random.permutation(np.resize(levels, k // 32))).repeat(32)
    a = np.empty((k // 512, 16))
    for p in range(k // 512):
        a[p, :8] = np.random.permutation(np.resize(levels, 8))
        for g in range(8):
            far = levels[np.abs(levels - a[p, g]) >= 10]
            a[p, g + 8] = far[np.random.randint(len(far))]
    return np.exp2(a.ravel()).repeat(32)


def f64(x):
    return np.asarray(x).astype(np.float64)


def striped(idx):
    return np.tile(idx.reshape(-1, 16).T, (8, 1)).astype(np.uint16)


def unstriped(offs):
    return offs[:16].T.reshape(-1).astype(np.int64)


def striped8(idx):
    return np.concatenate([x.reshape(-1, 16).T for x in idx]).astype(np.uint16)


def runs(offs, k):
    lists = np.stack([offs[16 * r : 16 * r + 16].T.reshape(-1) for r in range(8)]).astype(np.int64)
    return lists[np.arange(k) % 512 // 64]


def pack_weight(w):
    k, n = w.shape
    w = f64(np.asarray(w, np.float32).astype(ml_dtypes.bfloat16)).reshape(k // 32, 32, n)
    amax = np.abs(w).max(1)
    byte = np.clip(np.where(amax > 0, np.frexp(amax)[1] - 1 + 127 - 7, 1), 1, 254)
    scaled = (w * np.exp2(127.0 - byte)[:, None, :]).reshape(k, n).astype(np.float32)
    words = np.ascontiguousarray(scaled.reshape(k // 512, 128, 4, n).transpose(0, 1, 3, 2)).astype(ml_dtypes.float8_e4m3fn).view(np.uint8)
    return words, np.ascontiguousarray(byte.astype(np.uint8).reshape(k // 512, 16, n))


def unpack_weight(words, scales):
    g, p, n, _ = words.shape
    vals = np.ascontiguousarray(words).view(ml_dtypes.float8_e4m3fn).astype(np.float64) * np.repeat(np.exp2(scales.astype(np.float64) - 127.0), 8, axis=1)[..., None]
    return vals.transpose(0, 1, 3, 2).reshape(g * 512, n)


E2M1 = np.array([0.0, 0.5, 1.0, 1.5, 2.0, 3.0, 4.0, 6.0, -0.0, -0.5, -1.0, -1.5, -2.0, -3.0, -4.0, -6.0])


def pack_fp4(w):
    k, n = w.shape
    w = f64(np.asarray(w, np.float32).astype(ml_dtypes.bfloat16)).reshape(k // 32, 32, n)
    amax = np.abs(w).max(1)
    mant, ex = np.frexp(amax / 6.0)
    byte = np.clip(np.where(amax > 0, np.where(mant > 0.5, ex, ex - 1) + 127, 1), 1, 254)
    scaled = (w * np.exp2(127.0 - byte)[:, None, :]).reshape(k, n).astype(np.float32)
    c = np.ascontiguousarray(scaled.reshape(k // 512, 128, 4, n).transpose(0, 1, 3, 2)).astype(ml_dtypes.float4_e2m1fn).view(np.uint8) & 0xF
    words = (c[..., 0::2] | (c[..., 1::2] << 4)).reshape(k // 512, 128, 2 * n)
    return np.ascontiguousarray(words), np.ascontiguousarray(byte.astype(np.uint8).reshape(k // 512, 16, n))


def unpack_fp4(words, scales):
    g, _, n = scales.shape
    words = np.ascontiguousarray(words).reshape(g, 128, n, 2)
    nib = np.empty((g, 128, n, 4), np.uint8)
    nib[..., 0::2] = words & 0xF
    nib[..., 1::2] = words >> 4
    vals = E2M1[nib] * np.repeat(np.exp2(scales.astype(np.float64) - 127.0), 8, axis=1)[..., None]
    return vals.transpose(0, 1, 3, 2).reshape(g * 512, n)


def planes(y):
    n, m = y.shape
    v = y.astype(np.float32).astype(ml_dtypes.bfloat16).astype(np.float64).reshape(n // 32, 32, m)
    top = np.abs(v).max(1)
    byte = np.clip(np.where(top > 0, np.frexp(top)[1] - 1 + 127 - 7, 1), 1, 254)
    codes = (v * np.exp2(127.0 - byte)[:, None, :]).reshape(n, m).astype(np.float32).astype(ml_dtypes.float8_e4m3fn).view(np.uint8)
    words = codes.reshape(n // 512, 128, 4, m).transpose(0, 1, 3, 2)
    return np.ascontiguousarray(words), np.ascontiguousarray(byte.astype(np.uint8).reshape(n // 512, 16, m))


K, T, S, N, H, U = 512, 2048, 512, 512, 512, 1024


def setup_inputs():
    n = np.random.standard_normal
    s = mx_kscale(K)[:, None]
    u = mx_kscale(H)
    packed_xT = pack_weight(n((K, T)) * s)
    packed_w1 = pack_fp4(n((K, H)) / np.sqrt(K) / s)
    packed_w2 = pack_fp4(n((H, N)) / np.sqrt(H) / u[:, None])
    return {
        "x_words": packed_xT[0],
        "x_scales": packed_xT[1],
        "w1_words": packed_w1[0],
        "w1_scales": packed_w1[1],
        "gn": (np.random.uniform(0.5, 1.5, (H, 1)) * u[:, None]).astype(np.float32),
        "w2_words": packed_w2[0],
        "w2_scales": packed_w2[1],
        "mem": n((N, U)).astype(np.float32),
        "offs": striped(np.random.permutation(T)[:S]),
        "rt": striped8(np.stack([np.random.permutation(S) for _ in range(8)])),
        "lf": striped8(np.stack([np.random.permutation(S) for _ in range(8)])),
        "up": striped8(np.stack([np.random.permutation(S) for _ in range(8)])),
        "dn": striped8(np.stack([np.random.permutation(S) for _ in range(8)])),
        "slot": striped8(np.stack([np.random.permutation(U)[:S] for _ in range(8)])),
    }


def reference(x_words, x_scales, w1_words, w1_scales, gn, w2_words, w2_scales, mem, offs, rt, lf, up, dn, slot):
    xq = unpack_weight(x_words, x_scales)[:, unstriped(offs)]
    y = unpack_fp4(w1_words, w1_scales).T @ xq
    dx = y[np.arange(H)[:, None], runs(rt, H)] - (y[np.arange(H)[:, None], runs(lf, H)])
    dy = y[np.arange(H)[:, None], runs(up, H)] - (y[np.arange(H)[:, None], runs(dn, H)])
    z = f64(gn) * (np.sqrt(0.25 * ((dx) ** 2 + (dy) ** 2) + 0.05))
    h = unpack_fp4(w2_words, w2_scales).T @ mxq(z, 0, "e4m3")
    out = f64(mem).copy()
    out[np.arange(N)[:, None], runs(slot, N)] = h
    return (out,) + planes(out)

@@ -1,0 +1,244 @@
+from contextlib import ExitStack
+
+import concourse.mybir as mybir
+from concourse.masks import make_identity
+
+K, T, S, N, H, U = 512, 2048, 512, 512, 512, 1024
+FLOPS = 2 * K * H * S + 2 * H * N * S
+
+F32 = mybir.dt.float32
+BF16 = mybir.dt.bfloat16
+I32 = mybir.dt.int32
+U32 = mybir.dt.uint32
+U16 = mybir.dt.uint16
+U8 = mybir.dt.uint8
+FP8X4 = mybir.dt.float8_e4m3fn_x4
+FP4X4 = mybir.dt.float4_e2m1fn_x4
+ACT = mybir.ActivationFunctionType
+
+P = 128
+PACK = 4
+HALF = S // 2
+PIECE = 256
+
+
+def load_scale_rows(queue, plane, rows):
+    for q in range(4):
+        queue.dma_start(out=plane[32 * q : 32 * q + 4, :].bitcast(I32), in_=rows[4 * q : 4 * q + 4, :].bitcast(I32))
+
+
+def deal_weights(nc, words, raw_words, scales, raw_scales):
+    nc.vector.tensor_copy(
+        out=scales[:].rearrange("p (t m) -> p t m", t=PACK),
+        in_=raw_scales[:].rearrange("p (m t) -> p t m", t=PACK),
+    )
+    nc.vector.tensor_copy(
+        out=words[:].rearrange("p (t m b) -> p t m b", t=PACK, b=2),
+        in_=raw_words[:].rearrange("p (m t b) -> p t m b", t=PACK, b=2),
+    )
+
+
+def tile_picked_gradmag_none_po_kernel(
+    tc, x_words, x_scales, w1_words, w1_scales, gn, w2_words, w2_scales, mem, offs, rt, lf, up, dn, slot, out_0, out_1, out_2
+):
+    nc = tc.nc
+    with ExitStack() as ctx:
+        lists = ctx.enter_context(tc.tile_pool(name="lists", bufs=1))
+        keep = ctx.enter_context(tc.tile_pool(name="keep", bufs=1))
+        ring = ctx.enter_context(tc.tile_pool(name="ring", bufs=2))
+        prod = ctx.enter_context(tc.psum_pool(name="prod", bufs=1))
+        turn = ctx.enter_context(tc.psum_pool(name="turn", bufs=2))
+
+        xs_table = keep.tile([P, T], U8, name="xs_table", tag="xs_table", align_bytes=64)
+        w1s_raw = keep.tile([P, H], U8, name="w1s_raw", tag="w1s_raw", align_bytes=64)
+        w2s_raw = keep.tile([P, N], U8, name="w2s_raw", align_bytes=64)
+        nc.gpsimd.memset(xs_table[:].bitcast(I32), 0)
+        nc.gpsimd.memset(w1s_raw[:].bitcast(I32), 0)
+        nc.gpsimd.memset(w2s_raw[:].bitcast(I32), 0)
+
+        warm = keep.tile([P, 1], F32, name="warm")
+        nc.vector.memset(warm[:], 1.0)
+        warmed = keep.tile([P, 1], F32, name="warmed")
+        nc.scalar.activation(out=warmed[:], in_=warm[:], func=ACT.Sqrt, scale=0.25, bias=0.05)
+        offs_sb = lists.tile([P, S // 16], U16, name="offs_sb")
+        nc.sync.dma_start(offs_sb[:], offs)
+        w1w_raw = keep.tile([P, 2 * H], U8, name="w1w_raw", align_bytes=64)
+        nc.sync.dma_start(out=w1w_raw[:].bitcast(I32), in_=w1_words[0].bitcast(I32))
+        load_scale_rows(nc.sync, xs_table, x_scales[0])
+        xw_table = keep.tile([P, T], I32, name="xw_table", tag="slot0", align_bytes=64)
+        nc.sync.dma_start(out=xw_table[:], in_=x_words[0].rearrange("p n t -> p (n t)").bitcast(I32))
+        load_scale_rows(nc.sync, w1s_raw, w1_scales[0])
+        w2w_raw = keep.tile([P, 2 * N], U8, name="w2w_raw", tag="w2w_raw", align_bytes=64)
+        nc.sync.dma_start(out=w2w_raw[:].bitcast(I32), in_=w2_words[0].bitcast(I32))
+        near = []
+        for name, src in (("rt_sb", rt), ("lf_sb", lf), ("up_sb", up), ("dn_sb", dn)):
+            lst = lists.tile([P, S // 16], U16, name=name)
+            nc.sync.dma_start(lst[:], src)
+            near.append(lst)
+        load_scale_rows(nc.sync, w2s_raw, w2_scales[0])
+        gain = keep.tile([P, PACK], F32, name="gain")
+        nc.sync.dma_start(out=gain[:], in_=gn.rearrange("(p t) o -> p (t o)", t=PACK))
+        slot_sb = lists.tile([P, S // 16], U16, name="slot_sb")
+        nc.sync.dma_start(slot_sb[:], slot)
+
+        ident = keep.tile([P, P], F32, name="ident")
+        make_identity(nc, ident[:])
+
+        xs = keep.tile([P, S], U8, name="xs", tag="slot1", align_bytes=64)
+        nc.vector.tensor_copy(out=xs[:], in_=xs_table[:].indirect(offs_sb[:]))
+        w1w = keep.tile([P, 2 * H], U8, name="w1w", tag="slot2", align_bytes=64)
+        w1s = keep.tile([P, H], U8, name="w1s", align_bytes=64)
+        deal_weights(nc, w1w, w1w_raw, w1s, w1s_raw)
+        xw = []
+        for c, host in enumerate(("slot3", "w1s_raw")):
+            picked = keep.tile([P, HALF], U32, name=f"xw{c}", tag=host, align_bytes=64)
+            nc.vector.tensor_copy(
+                out=picked[:],
+                in_=xw_table[:].bitcast(U32).indirect(offs_sb[:, c * HALF // 16 : (c + 1) * HALF // 16]),
+            )
+            xw.append(picked)
+        w2w = keep.tile([P, 2 * N], U8, name="w2w", align_bytes=64)
+        w2s = keep.tile([P, N], U8, name="w2s", align_bytes=64)
+        deal_weights(nc, w2w, w2w_raw, w2s, w2s_raw)
+
+        y_pos, y_neg = [], []
+        for t in range(PACK):
+            pos = keep.tile([P, S], F32, name=f"y_pos{t}", tag=f"y_pos{t}")
+            neg = keep.tile([P, S], F32, name=f"y_neg{t}", tag=f"y_neg{t}")
+            halves = []
+            for c in range(2):
+                if c == 0:
+                    acc = prod.tile([P, HALF], F32, name=f"y_acc{t}", tag=f"prod{t}")
+                else:
+                    acc = turn.tile([P, HALF], F32, name=f"y_late{t}", tag=("diff", "total")[t % 2])
+                nc.tensor.matmul_mx(
+                    out=acc[:],
+                    lhsT=w1w[:, 2 * P * t : 2 * P * (t + 1)].bitcast(FP4X4),
+                    lhsT_scale=w1s[:, P * t : P * (t + 1)],
+                    rhs=xw[c][:].bitcast(FP8X4),
+                    rhs_scale=xs[:, HALF * c : HALF * (c + 1)],
+                    start=True,
+                    stop=True,
+                )
+                nc.scalar.copy(out=pos[:, HALF * c : HALF * (c + 1)], in_=acc[:])
+                halves.append(acc)
+            for c in range(2):
+                nc.scalar.activation(out=neg[:, HALF * c : HALF * (c + 1)], in_=halves[c][:], func=ACT.Copy, scale=-1.0)
+            y_pos.append(pos)
+            y_neg.append(neg)
+
+        mem_rows = mem.rearrange("(p t) u -> t p u", t=PACK)
+        out_rows = out_0.rearrange("(p t) u -> t p u", t=PACK)
+        page = []
+        for t in range(PACK):
+            win = keep.tile([P, U], F32, name=f"page{t}", tag=f"slot{t}", align_bytes=64)
+            nc.sync.dma_start(out=win[:], in_=mem_rows[t])
+            page.append(win)
+
+        h_acc = []
+        for c in range(2):
+            cols = slice(c * HALF // 16, (c + 1) * HALF // 16)
+            z_pairs = keep.tile([P, 2, HALF, 2], BF16, name=f"z_pairs{c}", tag=f"z_pairs{c}")
+            for t in range(PACK):
+                got = []
+                if (c, t) == (1, 2):
+                    after_first_half = keep.tile([P, 4, HALF], F32, name="got_held", tag="z_grouped0", align_bytes=64)
+                for k in range(4):
+                    if (c, t, k) == (0, 0, 0):
+                        g = keep.tile([P, HALF], F32, name="got_first", tag="w2w_raw", align_bytes=64)
+                        g = g[:]
+                    elif (c, t) == (1, 2):
+                        g = after_first_half[:, k, :]
+                    else:
+                        g = ring.tile([P, HALF], F32, name=f"got{k}", tag=f"got{k}")
+                        g = g[:]
+                    window = y_neg[t] if k % 2 else y_pos[t]
+                    nc.vector.tensor_copy(out=g, in_=window[:].indirect(near[k][:, cols]))
+                    got.append(g)
+                diff = turn.tile([P, 4, P], F32, name="diff")
+                for d in range(2):
+                    for b in range(2):
+                        for e in range(2):
+                            nc.tensor.matmul(
+                                diff[:, 2 * d + b, :],
+                                lhsT=got[2 * d + e][:, P * b : P * (b + 1)],
+                                rhs=ident[:],
+                                is_transpose=True,
+                                start=(e == 0),
+                                stop=(e == 1),
+                            )
+                squares = ring.tile([P, 4, P], F32, name="squares")
+                nc.scalar.activation(out=squares[:], in_=diff[:], func=ACT.Square)
+                total = turn.tile([P, HALF], F32, name="total")
+                for b in range(2):
+                    for d in range(2):
+                        nc.tensor.matmul(
+                            total[:, P * b : P * (b + 1)],
+                            lhsT=squares[:, 2 * d + b, :],
+                            rhs=ident[:],
+                            is_transpose=True,
+                            start=(d == 0),
+                            stop=(d == 1),
+                        )
+                root = keep.tile([P, HALF], F32, name=f"root{c}{t}", tag=f"root{t}")
+                nc.scalar.activation(out=root[:], in_=total[:], func=ACT.Sqrt, scale=0.25, bias=0.05)
+                nc.scalar.activation(out=z_pairs[:, t // 2, :, t % 2], in_=root[:], func=ACT.Copy, scale=gain[:, t : t + 1])
+            z_grouped = keep.tile([P, HALF * PACK], BF16, name=f"z_grouped{c}", tag=f"z_grouped{c}", align_bytes=64)
+            nc.scalar.copy(
+                out=z_grouped[:].bitcast(F32).rearrange("p (j u) -> p j u", u=2),
+                in_=z_pairs[:].rearrange("p u j e -> p (u j e)").bitcast(F32).rearrange("p (u j) -> p j u", u=2),
+            )
+            z_codes = ring.tile([P, HALF], U32, name="z_codes", align_bytes=64)
+            z_scales = ring.tile([P, HALF], U8, name="z_scales", align_bytes=64)
+            nc.vector.quantize_mx(out=z_codes[:].bitcast(FP8X4), scales=z_scales[:], in_=z_grouped[:])
+            accs = []
+            for t in range(PACK):
+                if c == 0:
+                    acc = prod.tile([P, HALF], F32, name=f"h_acc{t}", tag=f"prod{t}")
+                elif t % 2 == 0:
+                    acc = turn.tile([P, HALF], F32, name="h_late_a", tag="diff")
+                else:
+                    acc = turn.tile([P, HALF], F32, name="h_late_b", tag="total")
+                nc.tensor.matmul_mx(
+                    out=acc[:],
+                    lhsT=w2w[:, 2 * P * t : 2 * P * (t + 1)].bitcast(FP4X4),
+                    lhsT_scale=w2s[:, P * t : P * (t + 1)],
+                    rhs=z_codes[:].bitcast(FP8X4),
+                    rhs_scale=z_scales[:],
+                    start=True,
+                    stop=True,
+                )
+                accs.append(acc)
+            h_acc.append(accs)
+
+        first_two = keep.tile([P, 2, HALF], F32, name="h_first_two", tag="root1")
+        third = keep.tile([P, HALF], F32, name="h_third", tag="root2")
+        fourth = keep.tile([P, HALF], F32, name="h_fourth", tag="z_pairs1")
+        late = keep.tile([P, PACK, HALF], F32, name="h_late")
+        staged = [[first_two[:, 0, :], first_two[:, 1, :], third[:], fourth[:]], [late[:, t, :] for t in range(PACK)]]
+        for c in range(2):
+            cols = slice(c * HALF // 16, (c + 1) * HALF // 16)
+            for t in range(PACK):
+                nc.scalar.copy(out=staged[c][t], in_=h_acc[c][t][:])
+                nc.vector.tensor_copy(out=page[t][:].indirect(slot_sb[:, cols]), in_=staged[c][t])
+
+        pieces = U // PIECE
+        pairs = [keep.tile([P, 2, PIECE, 2], BF16, name=f"pairs{q}", align_bytes=64) for q in range(pieces)]
+        for t in range(PACK):
+            nc.sync.dma_start(out=out_rows[t], in_=page[t][:])
+            for q in range(pieces):
+                nc.scalar.copy(out=pairs[q][:, t // 2, :, t % 2], in_=page[t][:, PIECE * q : PIECE * (q + 1)])
+        out_scales = keep.tile([P, U], U8, name="out_scales", align_bytes=64)
+        out_words = out_1[0].rearrange("p n t -> p (n t)").bitcast(I32)
+        for q in range(pieces):
+            grouped = keep.tile([P, PIECE * PACK], BF16, name=f"grouped{q}", align_bytes=64)
+            nc.vector.tensor_copy(
+                out=grouped[:].bitcast(F32).rearrange("p (j u) -> p j u", u=2),
+                in_=pairs[q][:].rearrange("p u j e -> p (u j e)").bitcast(F32).rearrange("p (u j) -> p j u", u=2),
+            )
+            codes = keep.tile([P, PIECE], U32, name=f"codes{q}", align_bytes=64)
+            nc.vector.quantize_mx(out=codes[:].bitcast(FP8X4), scales=out_scales[:, PIECE * q : PIECE * (q + 1)], in_=grouped[:])
+            nc.sync.dma_start(out=out_words[:, PIECE * q : PIECE * (q + 1)], in_=codes[:].bitcast(I32))
+        for q in range(4):
+            queue = nc.sync if q % 2 else nc.scalar
+            queue.dma_start(out=out_2[0][4 * q : 4 * q + 4, :].bitcast(I32), in_=out_scales[32 * q : 32 * q + 4, :].bitcast(I32))

@@ -51,7 +51,7 @@ def tile_picked_gradmag_none_po_kernel(
 
         xs_table = keep.tile([P, T], U8, name="xs_table", tag="xs_table", align_bytes=64)
         w1s_raw = keep.tile([P, H], U8, name="w1s_raw", tag="w1s_raw", align_bytes=64)
-        w2s_raw = keep.tile([P, N], U8, name="w2s_raw", align_bytes=64)
+        w2s_raw = keep.tile([P, N], U8, name="w2s_raw", tag="w2s_raw", align_bytes=64)
         nc.gpsimd.memset(xs_table[:].bitcast(I32), 0)
         nc.gpsimd.memset(w1s_raw[:].bitcast(I32), 0)
         nc.gpsimd.memset(w2s_raw[:].bitcast(I32), 0)
@@ -103,16 +103,18 @@ def tile_picked_gradmag_none_po_kernel(
 
         y_pos, y_neg = [], []
         for t in range(PACK):
-            pos = keep.tile([P, S], F32, name=f"y_pos{t}", tag=f"y_pos{t}")
-            neg = keep.tile([P, S], F32, name=f"y_neg{t}", tag=f"y_neg{t}")
-            halves = []
+            pos = keep.tile([P, S], F32, name=f"y_pos{t}")
+            neg = keep.tile([P, S], F32, name=f"y_neg{t}")
+            if t == 0:
+                first = prod.tile([P, HALF], F32, name="y_first", tag="prod0")
+                second = prod.tile([P, HALF], F32, name="y_second", tag="prod1")
+                banks = [first[:], second[:]]
+            else:
+                acc = turn.tile([P, S], F32, name=f"y_acc{t}", tag="diff1" if t == PACK - 1 else "total")
+                banks = [acc[:, :HALF], acc[:, HALF:]]
             for c in range(2):
-                if c == 0:
-                    acc = prod.tile([P, HALF], F32, name=f"y_acc{t}", tag=f"prod{t}")
-                else:
-                    acc = turn.tile([P, HALF], F32, name=f"y_late{t}", tag=("diff", "total")[t % 2])
                 nc.tensor.matmul_mx(
-                    out=acc[:],
+                    out=banks[c],
                     lhsT=w1w[:, 2 * P * t : 2 * P * (t + 1)].bitcast(FP4X4),
                     lhsT_scale=w1s[:, P * t : P * (t + 1)],
                     rhs=xw[c][:].bitcast(FP8X4),
@@ -120,10 +122,14 @@ def tile_picked_gradmag_none_po_kernel(
                     start=True,
                     stop=True,
                 )
-                nc.scalar.copy(out=pos[:, HALF * c : HALF * (c + 1)], in_=acc[:])
-                halves.append(acc)
-            for c in range(2):
-                nc.scalar.activation(out=neg[:, HALF * c : HALF * (c + 1)], in_=halves[c][:], func=ACT.Copy, scale=-1.0)
+            if t == 0:
+                for c in range(2):
+                    nc.scalar.copy(out=pos[:, HALF * c : HALF * (c + 1)], in_=banks[c])
+                for c in range(2):
+                    nc.scalar.activation(out=neg[:, HALF * c : HALF * (c + 1)], in_=banks[c], func=ACT.Copy, scale=-1.0)
+            else:
+                nc.scalar.copy(out=pos[:], in_=acc[:])
+                nc.scalar.activation(out=neg[:], in_=acc[:], func=ACT.Copy, scale=-1.0)
             y_pos.append(pos)
             y_neg.append(neg)
 
@@ -142,45 +148,53 @@ def tile_picked_gradmag_none_po_kernel(
             for t in range(PACK):
                 got = []
                 if (c, t) == (1, 2):
-                    after_first_half = keep.tile([P, 4, HALF], F32, name="got_held", tag="z_grouped0", align_bytes=64)
+                    after_first_half = keep.tile([P, 6, HALF], F32, name="got_held", tag="z_grouped0", align_bytes=64)
                 for k in range(4):
                     if (c, t, k) == (0, 0, 0):
                         g = keep.tile([P, HALF], F32, name="got_first", tag="w2w_raw", align_bytes=64)
                         g = g[:]
-                    elif (c, t) == (1, 2):
-                        g = after_first_half[:, k, :]
+                    elif c == 1 and 4 * t + k >= 10:
+                        g = after_first_half[:, 4 * t + k - 10, :]
                     else:
                         g = ring.tile([P, HALF], F32, name=f"got{k}", tag=f"got{k}")
                         g = g[:]
                     window = y_neg[t] if k % 2 else y_pos[t]
                     nc.vector.tensor_copy(out=g, in_=window[:].indirect(near[k][:, cols]))
                     got.append(g)
-                diff = turn.tile([P, 4, P], F32, name="diff")
+                squares = []
+                if (c, t) == (1, 1):
+                    after_first_weave = keep.tile([P, 2, HALF], F32, name="squares_held", tag="z_pairs0")
                 for d in range(2):
+                    diff = turn.tile([P, HALF], F32, name=f"diff{d}", tag=f"diff{d}")
                     for b in range(2):
                         for e in range(2):
                             nc.tensor.matmul(
-                                diff[:, 2 * d + b, :],
+                                diff[:, P * b : P * (b + 1)],
                                 lhsT=got[2 * d + e][:, P * b : P * (b + 1)],
                                 rhs=ident[:],
                                 is_transpose=True,
                                 start=(e == 0),
                                 stop=(e == 1),
                             )
-                squares = ring.tile([P, 4, P], F32, name="squares")
-                nc.scalar.activation(out=squares[:], in_=diff[:], func=ACT.Square)
+                    if (c, t) == (1, 1):
+                        square = after_first_weave[:, d, :]
+                    else:
+                        square = ring.tile([P, HALF], F32, name=f"square{d}", tag=f"square{d}")
+                        square = square[:]
+                    nc.scalar.activation(out=square, in_=diff[:], func=ACT.Square)
+                    squares.append(square)
                 total = turn.tile([P, HALF], F32, name="total")
                 for b in range(2):
                     for d in range(2):
                         nc.tensor.matmul(
                             total[:, P * b : P * (b + 1)],
-                            lhsT=squares[:, 2 * d + b, :],
+                            lhsT=squares[d][:, P * b : P * (b + 1)],
                             rhs=ident[:],
                             is_transpose=True,
                             start=(d == 0),
                             stop=(d == 1),
                         )
-                root = keep.tile([P, HALF], F32, name=f"root{c}{t}", tag=f"root{t}")
+                root = ring.tile([P, HALF], F32, name="root")
                 nc.scalar.activation(out=root[:], in_=total[:], func=ACT.Sqrt, scale=0.25, bias=0.05)
                 nc.scalar.activation(out=z_pairs[:, t // 2, :, t % 2], in_=root[:], func=ACT.Copy, scale=gain[:, t : t + 1])
             z_grouped = keep.tile([P, HALF * PACK], BF16, name=f"z_grouped{c}", tag=f"z_grouped{c}", align_bytes=64)
@@ -193,14 +207,15 @@ def tile_picked_gradmag_none_po_kernel(
             nc.vector.quantize_mx(out=z_codes[:].bitcast(FP8X4), scales=z_scales[:], in_=z_grouped[:])
             accs = []
             for t in range(PACK):
-                if c == 0:
-                    acc = prod.tile([P, HALF], F32, name=f"h_acc{t}", tag=f"prod{t}")
-                elif t % 2 == 0:
-                    acc = turn.tile([P, HALF], F32, name="h_late_a", tag="diff")
+                if c == 1:
+                    bank = turn.tile([P, HALF], F32, name=f"h_late{t}", tag=f"diff{t % 2}")
+                    acc = bank[:]
                 else:
-                    acc = turn.tile([P, HALF], F32, name="h_late_b", tag="total")
+                    if t % 2 == 0:
+                        bank = prod.tile([P, 2, HALF], F32, name=f"h_early{t}", tag=f"prod{t // 2}")
+                    acc = bank[:, t % 2, :]
                 nc.tensor.matmul_mx(
-                    out=acc[:],
+                    out=acc,
                     lhsT=w2w[:, 2 * P * t : 2 * P * (t + 1)].bitcast(FP4X4),
                     lhsT_scale=w2s[:, P * t : P * (t + 1)],
                     rhs=z_codes[:].bitcast(FP8X4),
@@ -211,15 +226,14 @@ def tile_picked_gradmag_none_po_kernel(
                 accs.append(acc)
             h_acc.append(accs)
 
-        first_two = keep.tile([P, 2, HALF], F32, name="h_first_two", tag="root1")
-        third = keep.tile([P, HALF], F32, name="h_third", tag="root2")
+        early = keep.tile([P, PACK - 1, HALF], F32, name="h_early")
         fourth = keep.tile([P, HALF], F32, name="h_fourth", tag="z_pairs1")
         late = keep.tile([P, PACK, HALF], F32, name="h_late")
-        staged = [[first_two[:, 0, :], first_two[:, 1, :], third[:], fourth[:]], [late[:, t, :] for t in range(PACK)]]
+        staged = [[early[:, 0, :], early[:, 1, :], early[:, 2, :], fourth[:]], [late[:, t, :] for t in range(PACK)]]
         for c in range(2):
             cols = slice(c * HALF // 16, (c + 1) * HALF // 16)
             for t in range(PACK):
-                nc.scalar.copy(out=staged[c][t], in_=h_acc[c][t][:])
+                nc.scalar.copy(out=staged[c][t], in_=h_acc[c][t])
                 nc.vector.tensor_copy(out=page[t][:].indirect(slot_sb[:, cols]), in_=staged[c][t])
 
         pieces = U // PIECE
@@ -230,15 +244,20 @@ def tile_picked_gradmag_none_po_kernel(
                 nc.scalar.copy(out=pairs[q][:, t // 2, :, t % 2], in_=page[t][:, PIECE * q : PIECE * (q + 1)])
         out_scales = keep.tile([P, U], U8, name="out_scales", align_bytes=64)
         out_words = out_1[0].rearrange("p n t -> p (n t)").bitcast(I32)
+        codes = keep.tile([P, U], U32, name="codes", align_bytes=64)
+        stored = 0
         for q in range(pieces):
             grouped = keep.tile([P, PIECE * PACK], BF16, name=f"grouped{q}", align_bytes=64)
             nc.vector.tensor_copy(
                 out=grouped[:].bitcast(F32).rearrange("p (j u) -> p j u", u=2),
                 in_=pairs[q][:].rearrange("p u j e -> p (u j e)").bitcast(F32).rearrange("p (u j) -> p j u", u=2),
             )
-            codes = keep.tile([P, PIECE], U32, name=f"codes{q}", align_bytes=64)
-            nc.vector.quantize_mx(out=codes[:].bitcast(FP8X4), scales=out_scales[:, PIECE * q : PIECE * (q + 1)], in_=grouped[:])
-            nc.sync.dma_start(out=out_words[:, PIECE * q : PIECE * (q + 1)], in_=codes[:].bitcast(I32))
+            cols = slice(PIECE * q, PIECE * (q + 1))
+            nc.vector.quantize_mx(out=codes[:, cols].bitcast(FP8X4), scales=out_scales[:, cols], in_=grouped[:])
+            if q > 0:
+                ready = slice(stored, PIECE * (q + 1))
+                nc.sync.dma_start(out=out_words[:, ready], in_=codes[:, ready].bitcast(I32))
+                stored = PIECE * (q + 1)
         for q in range(4):
             queue = nc.sync if q % 2 else nc.scalar
             queue.dma_start(out=out_2[0][4 * q : 4 * q + 4, :].bitcast(I32), in_=out_scales[32 * q : 32 * q + 4, :].bitcast(I32))

from contextlib import ExitStack

import concourse.mybir as mybir
from concourse.masks import make_identity

K, T, S, N, H, U = 512, 2048, 512, 512, 512, 1024
FLOPS = 2 * K * H * S + 2 * H * N * S

F32 = mybir.dt.float32
BF16 = mybir.dt.bfloat16
I32 = mybir.dt.int32
U32 = mybir.dt.uint32
U16 = mybir.dt.uint16
U8 = mybir.dt.uint8
FP8X4 = mybir.dt.float8_e4m3fn_x4
FP4X4 = mybir.dt.float4_e2m1fn_x4
ACT = mybir.ActivationFunctionType

P = 128
PACK = 4
HALF = S // 2
PIECE = 256


def load_scale_rows(queue, plane, rows):
    for q in range(4):
        queue.dma_start(out=plane[32 * q : 32 * q + 4, :].bitcast(I32), in_=rows[4 * q : 4 * q + 4, :].bitcast(I32))


def deal_weights(nc, words, raw_words, scales, raw_scales):
    nc.vector.tensor_copy(
        out=scales[:].rearrange("p (t m) -> p t m", t=PACK),
        in_=raw_scales[:].rearrange("p (m t) -> p t m", t=PACK),
    )
    nc.vector.tensor_copy(
        out=words[:].rearrange("p (t m b) -> p t m b", t=PACK, b=2),
        in_=raw_words[:].rearrange("p (m t b) -> p t m b", t=PACK, b=2),
    )


def tile_picked_gradmag_none_po_kernel(
    tc, x_words, x_scales, w1_words, w1_scales, gn, w2_words, w2_scales, mem, offs, rt, lf, up, dn, slot, out_0, out_1, out_2
):
    nc = tc.nc
    with ExitStack() as ctx:
        lists = ctx.enter_context(tc.tile_pool(name="lists", bufs=1))
        keep = ctx.enter_context(tc.tile_pool(name="keep", bufs=1))
        ring = ctx.enter_context(tc.tile_pool(name="ring", bufs=2))
        prod = ctx.enter_context(tc.psum_pool(name="prod", bufs=1))
        turn = ctx.enter_context(tc.psum_pool(name="turn", bufs=2))

        xs_table = keep.tile([P, T], U8, name="xs_table", tag="xs_table", align_bytes=64)
        w1s_raw = keep.tile([P, H], U8, name="w1s_raw", tag="w1s_raw", align_bytes=64)
        w2s_raw = keep.tile([P, N], U8, name="w2s_raw", tag="w2s_raw", align_bytes=64)
        nc.gpsimd.memset(xs_table[:].bitcast(I32), 0)
        nc.gpsimd.memset(w1s_raw[:].bitcast(I32), 0)
        nc.gpsimd.memset(w2s_raw[:].bitcast(I32), 0)

        warm = keep.tile([P, 1], F32, name="warm")
        nc.vector.memset(warm[:], 1.0)
        warmed = keep.tile([P, 1], F32, name="warmed")
        nc.scalar.activation(out=warmed[:], in_=warm[:], func=ACT.Sqrt, scale=0.25, bias=0.05)
        offs_sb = lists.tile([P, S // 16], U16, name="offs_sb")
        nc.sync.dma_start(offs_sb[:], offs)
        w1w_raw = keep.tile([P, 2 * H], U8, name="w1w_raw", align_bytes=64)
        nc.sync.dma_start(out=w1w_raw[:].bitcast(I32), in_=w1_words[0].bitcast(I32))
        load_scale_rows(nc.sync, xs_table, x_scales[0])
        xw_table = keep.tile([P, T], I32, name="xw_table", tag="slot0", align_bytes=64)
        nc.sync.dma_start(out=xw_table[:], in_=x_words[0].rearrange("p n t -> p (n t)").bitcast(I32))
        load_scale_rows(nc.sync, w1s_raw, w1_scales[0])
        w2w_raw = keep.tile([P, 2 * N], U8, name="w2w_raw", tag="w2w_raw", align_bytes=64)
        nc.sync.dma_start(out=w2w_raw[:].bitcast(I32), in_=w2_words[0].bitcast(I32))
        near = []
        for name, src in (("rt_sb", rt), ("lf_sb", lf), ("up_sb", up), ("dn_sb", dn)):
            lst = lists.tile([P, S // 16], U16, name=name)
            nc.sync.dma_start(lst[:], src)
            near.append(lst)
        load_scale_rows(nc.sync, w2s_raw, w2_scales[0])
        gain = keep.tile([P, PACK], F32, name="gain")
        nc.sync.dma_start(out=gain[:], in_=gn.rearrange("(p t) o -> p (t o)", t=PACK))
        slot_sb = lists.tile([P, S // 16], U16, name="slot_sb")
        nc.sync.dma_start(slot_sb[:], slot)

        ident = keep.tile([P, P], F32, name="ident")
        make_identity(nc, ident[:])

        xs = keep.tile([P, S], U8, name="xs", tag="slot1", align_bytes=64)
        nc.vector.tensor_copy(out=xs[:], in_=xs_table[:].indirect(offs_sb[:]))
        w1w = keep.tile([P, 2 * H], U8, name="w1w", tag="slot2", align_bytes=64)
        w1s = keep.tile([P, H], U8, name="w1s", align_bytes=64)
        deal_weights(nc, w1w, w1w_raw, w1s, w1s_raw)
        xw = []
        for c, host in enumerate(("slot3", "w1s_raw")):
            picked = keep.tile([P, HALF], U32, name=f"xw{c}", tag=host, align_bytes=64)
            nc.vector.tensor_copy(
                out=picked[:],
                in_=xw_table[:].bitcast(U32).indirect(offs_sb[:, c * HALF // 16 : (c + 1) * HALF // 16]),
            )
            xw.append(picked)
        w2w = keep.tile([P, 2 * N], U8, name="w2w", align_bytes=64)
        w2s = keep.tile([P, N], U8, name="w2s", align_bytes=64)
        deal_weights(nc, w2w, w2w_raw, w2s, w2s_raw)

        y_pos, y_neg = [], []
        for t in range(PACK):
            pos = keep.tile([P, S], F32, name=f"y_pos{t}")
            neg = keep.tile([P, S], F32, name=f"y_neg{t}")
            if t == 0:
                first = prod.tile([P, HALF], F32, name="y_first", tag="prod0")
                second = prod.tile([P, HALF], F32, name="y_second", tag="prod1")
                banks = [first[:], second[:]]
            else:
                acc = turn.tile([P, S], F32, name=f"y_acc{t}", tag="diff1" if t == PACK - 1 else "total")
                banks = [acc[:, :HALF], acc[:, HALF:]]
            for c in range(2):
                nc.tensor.matmul_mx(
                    out=banks[c],
                    lhsT=w1w[:, 2 * P * t : 2 * P * (t + 1)].bitcast(FP4X4),
                    lhsT_scale=w1s[:, P * t : P * (t + 1)],
                    rhs=xw[c][:].bitcast(FP8X4),
                    rhs_scale=xs[:, HALF * c : HALF * (c + 1)],
                    start=True,
                    stop=True,
                )
            if t == 0:
                for c in range(2):
                    nc.scalar.copy(out=pos[:, HALF * c : HALF * (c + 1)], in_=banks[c])
                for c in range(2):
                    nc.scalar.activation(out=neg[:, HALF * c : HALF * (c + 1)], in_=banks[c], func=ACT.Copy, scale=-1.0)
            else:
                nc.scalar.copy(out=pos[:], in_=acc[:])
                nc.scalar.activation(out=neg[:], in_=acc[:], func=ACT.Copy, scale=-1.0)
            y_pos.append(pos)
            y_neg.append(neg)

        mem_rows = mem.rearrange("(p t) u -> t p u", t=PACK)
        out_rows = out_0.rearrange("(p t) u -> t p u", t=PACK)
        page = []
        for t in range(PACK):
            win = keep.tile([P, U], F32, name=f"page{t}", tag=f"slot{t}", align_bytes=64)
            nc.sync.dma_start(out=win[:], in_=mem_rows[t])
            page.append(win)

        h_acc = []
        for c in range(2):
            cols = slice(c * HALF // 16, (c + 1) * HALF // 16)
            z_pairs = keep.tile([P, 2, HALF, 2], BF16, name=f"z_pairs{c}", tag=f"z_pairs{c}")
            for t in range(PACK):
                got = []
                if (c, t) == (1, 2):
                    after_first_half = keep.tile([P, 6, HALF], F32, name="got_held", tag="z_grouped0", align_bytes=64)
                for k in range(4):
                    if (c, t, k) == (0, 0, 0):
                        g = keep.tile([P, HALF], F32, name="got_first", tag="w2w_raw", align_bytes=64)
                        g = g[:]
                    elif c == 1 and 4 * t + k >= 10:
                        g = after_first_half[:, 4 * t + k - 10, :]
                    else:
                        g = ring.tile([P, HALF], F32, name=f"got{k}", tag=f"got{k}")
                        g = g[:]
                    window = y_neg[t] if k % 2 else y_pos[t]
                    nc.vector.tensor_copy(out=g, in_=window[:].indirect(near[k][:, cols]))
                    got.append(g)
                squares = []
                if (c, t) == (1, 1):
                    after_first_weave = keep.tile([P, 2, HALF], F32, name="squares_held", tag="z_pairs0")
                for d in range(2):
                    diff = turn.tile([P, HALF], F32, name=f"diff{d}", tag=f"diff{d}")
                    for b in range(2):
                        for e in range(2):
                            nc.tensor.matmul(
                                diff[:, P * b : P * (b + 1)],
                                lhsT=got[2 * d + e][:, P * b : P * (b + 1)],
                                rhs=ident[:],
                                is_transpose=True,
                                start=(e == 0),
                                stop=(e == 1),
                            )
                    if (c, t) == (1, 1):
                        square = after_first_weave[:, d, :]
                    else:
                        square = ring.tile([P, HALF], F32, name=f"square{d}", tag=f"square{d}")
                        square = square[:]
                    nc.scalar.activation(out=square, in_=diff[:], func=ACT.Square)
                    squares.append(square)
                total = turn.tile([P, HALF], F32, name="total")
                for b in range(2):
                    for d in range(2):
                        nc.tensor.matmul(
                            total[:, P * b : P * (b + 1)],
                            lhsT=squares[d][:, P * b : P * (b + 1)],
                            rhs=ident[:],
                            is_transpose=True,
                            start=(d == 0),
                            stop=(d == 1),
                        )
                root = ring.tile([P, HALF], F32, name="root")
                nc.scalar.activation(out=root[:], in_=total[:], func=ACT.Sqrt, scale=0.25, bias=0.05)
                nc.scalar.activation(out=z_pairs[:, t // 2, :, t % 2], in_=root[:], func=ACT.Copy, scale=gain[:, t : t + 1])
            z_grouped = keep.tile([P, HALF * PACK], BF16, name=f"z_grouped{c}", tag=f"z_grouped{c}", align_bytes=64)
            nc.scalar.copy(
                out=z_grouped[:].bitcast(F32).rearrange("p (j u) -> p j u", u=2),
                in_=z_pairs[:].rearrange("p u j e -> p (u j e)").bitcast(F32).rearrange("p (u j) -> p j u", u=2),
            )
            z_codes = ring.tile([P, HALF], U32, name="z_codes", align_bytes=64)
            z_scales = ring.tile([P, HALF], U8, name="z_scales", align_bytes=64)
            nc.vector.quantize_mx(out=z_codes[:].bitcast(FP8X4), scales=z_scales[:], in_=z_grouped[:])
            accs = []
            for t in range(PACK):
                if c == 1:
                    bank = turn.tile([P, HALF], F32, name=f"h_late{t}", tag=f"diff{t % 2}")
                    acc = bank[:]
                else:
                    if t % 2 == 0:
                        bank = prod.tile([P, 2, HALF], F32, name=f"h_early{t}", tag=f"prod{t // 2}")
                    acc = bank[:, t % 2, :]
                nc.tensor.matmul_mx(
                    out=acc,
                    lhsT=w2w[:, 2 * P * t : 2 * P * (t + 1)].bitcast(FP4X4),
                    lhsT_scale=w2s[:, P * t : P * (t + 1)],
                    rhs=z_codes[:].bitcast(FP8X4),
                    rhs_scale=z_scales[:],
                    start=True,
                    stop=True,
                )
                accs.append(acc)
            h_acc.append(accs)

        early = keep.tile([P, PACK - 1, HALF], F32, name="h_early")
        fourth = keep.tile([P, HALF], F32, name="h_fourth", tag="z_pairs1")
        late = keep.tile([P, PACK, HALF], F32, name="h_late")
        staged = [[early[:, 0, :], early[:, 1, :], early[:, 2, :], fourth[:]], [late[:, t, :] for t in range(PACK)]]
        for c in range(2):
            cols = slice(c * HALF // 16, (c + 1) * HALF // 16)
            for t in range(PACK):
                nc.scalar.copy(out=staged[c][t], in_=h_acc[c][t])
                nc.vector.tensor_copy(out=page[t][:].indirect(slot_sb[:, cols]), in_=staged[c][t])

        pieces = U // PIECE
        pairs = [keep.tile([P, 2, PIECE, 2], BF16, name=f"pairs{q}", align_bytes=64) for q in range(pieces)]
        for t in range(PACK):
            nc.sync.dma_start(out=out_rows[t], in_=page[t][:])
            for q in range(pieces):
                nc.scalar.copy(out=pairs[q][:, t // 2, :, t % 2], in_=page[t][:, PIECE * q : PIECE * (q + 1)])
        out_scales = keep.tile([P, U], U8, name="out_scales", align_bytes=64)
        out_words = out_1[0].rearrange("p n t -> p (n t)").bitcast(I32)
        codes = keep.tile([P, U], U32, name="codes", align_bytes=64)
        stored = 0
        for q in range(pieces):
            grouped = keep.tile([P, PIECE * PACK], BF16, name=f"grouped{q}", align_bytes=64)
            nc.vector.tensor_copy(
                out=grouped[:].bitcast(F32).rearrange("p (j u) -> p j u", u=2),
                in_=pairs[q][:].rearrange("p u j e -> p (u j e)").bitcast(F32).rearrange("p (u j) -> p j u", u=2),
            )
            cols = slice(PIECE * q, PIECE * (q + 1))
            nc.vector.quantize_mx(out=codes[:, cols].bitcast(FP8X4), scales=out_scales[:, cols], in_=grouped[:])
            if q > 0:
                ready = slice(stored, PIECE * (q + 1))
                nc.sync.dma_start(out=out_words[:, ready], in_=codes[:, ready].bitcast(I32))
                stored = PIECE * (q + 1)
        for q in range(4):
            queue = nc.sync if q % 2 else nc.scalar
            queue.dma_start(out=out_2[0][4 * q : 4 * q + 4, :].bitcast(I32), in_=out_scales[32 * q : 32 * q + 4, :].bitcast(I32))
